import numpy as np
import ml_dtypes


def mxq(x, axis, fmt="e4m3"):
    dtype, down = {"e4m3": (ml_dtypes.float8_e4m3fn, 7), "e5m2": (ml_dtypes.float8_e5m2, 14)}[fmt]
    v = np.moveaxis(np.asarray(x, np.float32).astype(ml_dtypes.bfloat16).astype(np.float64), axis, -1)
    blocks = v.reshape(v.shape[:-1] + (-1, 32))
    amax = np.abs(blocks).max(-1, keepdims=True)
    byte = np.maximum(np.where(amax > 0, np.frexp(amax)[1] - 1 + 127, 0) - down, 1)
    scale = np.exp2(byte - 127.0)
    codes = (blocks / scale).astype(np.float32).astype(dtype).astype(np.float64)
    return np.moveaxis((codes * scale).reshape(v.shape), -1, axis)


WIDE = False


def mx_kscale(k):
    if not WIDE:
        return np.ones(k)
    levels = np.array([10, -10, 5, -5, 0])
    if k % 512:
        return np.exp2(np.random.permutation(np.resize(levels, k // 32))).repeat(32)
    a = np.empty((k // 512, 16))
    for p in range(k // 512):
        a[p, :8] = np.random.permutation(np.resize(levels, 8))
        for g in range(8):
            far = levels[np.abs(levels - a[p, g]) >= 10]
            a[p, g + 8] = far[np.random.randint(len(far))]
    return np.exp2(a.ravel()).repeat(32)


def f64(x):
    return np.asarray(x).astype(np.float64)


def striped8(idx):
    return np.asarray(idx).reshape(8, -1, 16).transpose(0, 2, 1).reshape(128, -1).astype(np.uint16)


def unstriped8(offs):
    return offs.reshape(8, 16, -1).transpose(0, 2, 1).reshape(8, -1).astype(np.int64)


def pick8(x, idx, run):
    r = np.arange(len(x))
    return x[r[:, None], idx[r % (8 * run) // run]]


E2M1 = np.array([0.0, 0.5, 1.0, 1.5, 2.0, 3.0, 4.0, 6.0, -0.0, -0.5, -1.0, -1.5, -2.0, -3.0, -4.0, -6.0])


def pack_weight(w, fmt):
    k, n = w.shape
    w = f64(np.asarray(w, np.float32).astype(ml_dtypes.bfloat16)).reshape(k // 32, 32, n)
    amax = np.abs(w).max(1)
    if fmt == "e4m3":
        byte = np.frexp(amax)[1] - 1 + 127 - 7
    else:
        mant, ex = np.frexp(amax / 6.0)
        byte = np.where(mant > 0.5, ex, ex - 1) + 127
    byte = np.clip(np.where(amax > 0, byte, 1), 1, 254)
    scaled = (w * np.exp2(127.0 - byte)[:, None, :]).reshape(k, n).astype(np.float32)
    by_word = np.ascontiguousarray(scaled.reshape(k // 512, 128, 4, n).transpose(0, 1, 3, 2))
    if fmt == "e4m3":
        words = by_word.astype(ml_dtypes.float8_e4m3fn).view(np.uint8)
    else:
        c = by_word.astype(ml_dtypes.float4_e2m1fn).view(np.uint8) & 0xF
        words = (c[..., 0::2] | (c[..., 1::2] << 4)).reshape(k // 512, 128, 2 * n)
    return np.ascontiguousarray(words), np.ascontiguousarray(byte.astype(np.uint8).reshape(k // 512, 16, n))


def unpack_weight(words, scales, fmt):
    g, _, n = scales.shape
    words = np.ascontiguousarray(words).reshape(g, 128, n, -1)
    if fmt == "e4m3":
        vals = words.view(ml_dtypes.float8_e4m3fn).astype(np.float64)
    else:
        nib = np.empty((g, 128, n, 4), np.uint8)
        nib[..., 0::2] = words & 0xF
        nib[..., 1::2] = words >> 4
        vals = E2M1[nib]
    vals = vals * np.repeat(np.exp2(scales.astype(np.float64) - 127.0), 8, axis=1)[..., None]
    return vals.transpose(0, 1, 3, 2).reshape(g * 512, n)


D, K, T, I, Q = 512, 512, 1024, 512, 128


def setup_inputs():
    n = np.random.standard_normal
    idx = np.stack([np.random.permutation(T)[:I] for _ in range(8)])
    idx2 = np.stack([np.random.permutation(T)[:I] for _ in range(8)])
    idx3 = np.stack([np.random.permutation(T)[:I] for _ in range(8)])
    idx4 = np.stack([np.random.permutation(T)[:I] for _ in range(8)])
    idx5 = np.stack([np.random.permutation(T)[:I] for _ in range(8)])
    fd = mx_kscale(D)
    fk = mx_kscale(K)
    wqp = pack_weight(n((D, K)) * 1.0 / np.sqrt(D) * fd[:, None] * fk, "e4m3")
    cachep = pack_weight(n((K, T)) * 1.0 / np.sqrt(K) / fk[:, None], "e2m1")
    tagsp = pack_weight(n((D, T)) * 0.5 / np.sqrt(D) * fd[:, None], "e4m3")
    return {
        "states": (n((D, Q)) * 0.95 / fd[:, None]).astype(np.float32),
        "wq_words": wqp[0],
        "wq_scales": wqp[1],
        "cache_words": cachep[0],
        "cache_scales": cachep[1],
        "tags_words": tagsp[0],
        "tags_scales": tagsp[1],
        "offs": striped8(idx),
        "offs2": striped8(idx2),
        "offs3": striped8(idx3),
        "offs4": striped8(idx4),
        "offs5": striped8(idx5),
    }


def reference(states, wq_words, wq_scales, cache_words, cache_scales, tags_words, tags_scales, offs, offs2, offs3, offs4, offs5):
    idx = unstriped8(offs)
    idx2 = unstriped8(offs2)
    idx3 = unstriped8(offs3)
    idx4 = unstriped8(offs4)
    idx5 = unstriped8(offs5)
    wqu = unpack_weight(wq_words, wq_scales, "e4m3")
    cacheu = unpack_weight(cache_words, cache_scales, "e2m1")
    tagsu = unpack_weight(tags_words, tags_scales, "e4m3")
    statesq = mxq(f64(states), 0, "e4m3")
    qv = wqu.T @ statesq
    qvq = mxq(qv, 0, "e4m3")
    a = qvq.T @ cacheu + statesq.T @ tagsu
    f1 = np.zeros((Q, T))
    f1[np.arange(Q)[:, None], idx2[np.arange(Q) % 128 // 16]] = pick8(a, idx, 16)
    m1 = np.maximum(a, f1)
    n1 = np.minimum(a, f1)
    w = pick8(m1, idx3, 16) + pick8(n1, idx4, 16)
    f2 = np.zeros((Q, T))
    f2[np.arange(Q)[:, None], idx5[np.arange(Q) % 128 // 16]] = w
    c2 = m1 - f2
    y = np.maximum(pick8(c2, idx3, 16), pick8(n1, idx, 16))
    return y

@@ -1,0 +1,167 @@
+from contextlib import ExitStack
+
+import concourse.mybir as mybir
+
+F32 = mybir.dt.float32
+BF16 = mybir.dt.bfloat16
+I32 = mybir.dt.int32
+U32 = mybir.dt.uint32
+U16 = mybir.dt.uint16
+U8 = mybir.dt.uint8
+FP8X4 = mybir.dt.float8_e4m3fn_x4
+FP4X4 = mybir.dt.float4_e2m1fn_x4
+ALU = mybir.AluOpType
+COPY = mybir.ActivationFunctionType.Copy
+
+P = 128
+PACK = 4
+D = K = 512
+T = 1024
+SLOTS = 512
+Q = 128
+QUADRANTS = 4
+LIVE = 4
+N_BANK = 256
+HALF = SLOTS // 2
+Q_VECTOR = 88
+
+FLOPS = 2 * D * K * Q + 2 * K * Q * T + 2 * D * Q * T
+
+
+def tile_attend_revisit_parts_kernel(tc, states, wq_words, wq_scales, cache_words, cache_scales,
+                                      tags_words, tags_scales, offs, offs2, offs3, offs4, offs5, out):
+    nc = tc.nc
+    with ExitStack() as ctx:
+        sb = ctx.enter_context(tc.tile_pool(name="sb", bufs=1))
+        ps = ctx.enter_context(tc.psum_pool(name="ps", bufs=1))
+
+        def stage_scales(queue, scales, width, name):
+            staged = sb.tile([LIVE, QUADRANTS, width // 4], I32, name=name)
+            queue.dma_start(out=staged[:], in_=scales[0].bitcast(I32).rearrange("(g r) c -> r g c", r=LIVE))
+            return staged
+
+        def zeroed_plane(width, name):
+            plane = sb.tile([P, width], U8, align_bytes=64, name=name)
+            nc.vector.memset(plane[:].bitcast(I32), 0)
+            return plane
+
+        def spread_scales(plane, staged):
+            for g in range(QUADRANTS):
+                nc.vector.tensor_copy(out=plane[32 * g : 32 * g + LIVE, :].bitcast(I32), in_=staged[:, g, :])
+
+        def entries(lists, half):
+            return lists[:, half * HALF // 16 : (half + 1) * HALF // 16]
+
+        def slots(half):
+            return slice(half * HALF, (half + 1) * HALF)
+
+        wq_staged = stage_scales(nc.scalar, wq_scales, K, "wq_staged")
+        states_raw = sb.tile([P, PACK, Q], F32, name="states_raw")
+        nc.sync.dma_start(out=states_raw[:], in_=states.rearrange("(p j) q -> p j q", j=PACK))
+        wq_codes = sb.tile([P, K], I32, align_bytes=64, name="wq_codes")
+        nc.sync.dma_start(out=wq_codes[:], in_=wq_words[0].rearrange("p n t -> p (n t)").bitcast(I32))
+        tags_staged = stage_scales(nc.sync, tags_scales, T, "tags_staged")
+        cache_staged = stage_scales(nc.sync, cache_scales, T, "cache_staged")
+        tags_codes = sb.tile([P, T], I32, align_bytes=64, name="tags_codes")
+        nc.sync.dma_start(out=tags_codes[:], in_=tags_words[0].rearrange("p n t -> p (n t)").bitcast(I32))
+        cache_codes = sb.tile([P, 2 * T], U8, align_bytes=64, name="cache_codes")
+        nc.sync.dma_start(out=cache_codes[:].bitcast(I32), in_=cache_words[0].bitcast(I32))
+        lists = []
+        for number, source in enumerate((offs, offs2, offs3, offs4, offs5)):
+            held = sb.tile([P, SLOTS // 16], U16, name="list%d" % number)
+            nc.sync.dma_start(held[:], source)
+            lists.append(held)
+        idx, idx2, idx3, idx4, idx5 = lists
+
+        wq_plane = zeroed_plane(K, "wq_plane")
+        tags_plane = zeroed_plane(T, "tags_plane")
+        cache_plane = zeroed_plane(T, "cache_plane")
+        f1 = sb.tile([P, T], F32, name="f1")
+        nc.vector.memset(f1[:], 0.0)
+        f2 = sb.tile([P, T], F32, name="f2")
+        nc.vector.memset(f2[:], 0.0)
+
+        spread_scales(wq_plane, wq_staged)
+
+        states_bf = sb.tile([P, Q, PACK], BF16, align_bytes=64, name="states_bf")
+        lo, hi = slice(0, Q_VECTOR), slice(Q_VECTOR, Q)
+        nc.vector.tensor_copy(out=states_bf[:, lo, :].rearrange("p (c i) j -> p c j i", i=4),
+                              in_=states_raw[:, :, lo].rearrange("p j (c i) -> p c j i", i=4))
+        nc.scalar.activation(states_bf[:, hi, :].rearrange("p (c i) j -> p c j i", i=4),
+                             states_raw[:, :, hi].rearrange("p j (c i) -> p c j i", i=4), COPY)
+
+        wq_plane_dealt = sb.tile([P, K], U8, align_bytes=64, name="wq_plane_dealt")
+        nc.vector.tensor_copy(out=wq_plane_dealt[:].rearrange("p (t c i) -> p c t i", t=PACK, i=16),
+                              in_=wq_plane[:].rearrange("p (c i t) -> p c t i", t=PACK, i=16))
+        wq_dealt = sb.tile([P, K], U32, align_bytes=64, name="wq_dealt")
+        nc.scalar.copy(wq_dealt[:].rearrange("p (t c i) -> p c t i", t=PACK, i=4),
+                       wq_codes[:].bitcast(U32).rearrange("p (c i t) -> p c t i", t=PACK, i=4))
+
+        states_codes = sb.tile([P, Q], U32, align_bytes=64, name="states_codes")
+        states_plane = sb.tile([P, Q], U8, align_bytes=64, name="states_plane")
+        nc.vector.quantize_mx(out=states_codes[:].bitcast(FP8X4), scales=states_plane[:],
+                              in_=states_bf[:].rearrange("p q j -> p (q j)"))
+
+        qv_ps = ps.tile([P, PACK, Q], F32, name="qv_ps")
+        for t in range(PACK):
+            cols = slice(t * P, (t + 1) * P)
+            nc.tensor.matmul_mx(out=qv_ps[:, t, :], lhsT=wq_dealt[:, cols].bitcast(FP8X4),
+                                lhsT_scale=wq_plane_dealt[:, cols], rhs=states_codes[:].bitcast(FP8X4),
+                                rhs_scale=states_plane[:], start=True, stop=True)
+        qv_bf = sb.tile([P, Q, PACK], BF16, align_bytes=64, name="qv_bf")
+        nc.scalar.copy(qv_bf[:], qv_ps[:].rearrange("p t q -> p q t"))
+
+        spread_scales(tags_plane, tags_staged)
+        banks = [ps.tile([P, N_BANK], F32, name="a_ps%d" % b) for b in range(T // N_BANK)]
+        for b, bank in enumerate(banks):
+            cols = slice(b * N_BANK, (b + 1) * N_BANK)
+            nc.tensor.matmul_mx(out=bank[:], lhsT=states_codes[:].bitcast(FP8X4), lhsT_scale=states_plane[:],
+                                rhs=tags_codes[:, cols].bitcast(FP8X4), rhs_scale=tags_plane[:, cols],
+                                start=True, stop=False)
+        spread_scales(cache_plane, cache_staged)
+
+        qv_codes = sb.tile([P, Q], U32, align_bytes=64, name="qv_codes")
+        qv_plane = sb.tile([P, Q], U8, align_bytes=64, name="qv_plane")
+        nc.vector.quantize_mx(out=qv_codes[:].bitcast(FP8X4), scales=qv_plane[:],
+                              in_=qv_bf[:].rearrange("p q t -> p (q t)"))
+
+        a = sb.tile([P, T], F32, name="a")
+        for b, bank in enumerate(banks):
+            cols = slice(b * N_BANK, (b + 1) * N_BANK)
+            nc.tensor.matmul_mx(out=bank[:], lhsT=qv_codes[:].bitcast(FP8X4), lhsT_scale=qv_plane[:],
+                                rhs=cache_codes[:, 2 * b * N_BANK : 2 * (b + 1) * N_BANK].bitcast(FP4X4),
+                                rhs_scale=cache_plane[:, cols], start=False, stop=True)
+            if b % 2 == 0:
+                nc.scalar.copy(a[:, cols], bank[:])
+            else:
+                nc.vector.tensor_copy(out=a[:, cols], in_=bank[:])
+
+        picked = [sb.tile([P, HALF], F32, name="picked%d" % h) for h in range(2)]
+        for h in range(2):
+            nc.vector.tensor_copy(out=picked[h][:], in_=a[:].indirect(entries(idx, h)))
+            nc.scalar.activation(f1[:].indirect(entries(idx2, h)), picked[h][:], COPY)
+
+        m1 = sb.tile([P, T], F32, name="m1")
+        n1 = sb.tile([P, T], F32, name="n1")
+        nc.vector.tensor_tensor(m1[:], a[:], f1[:], ALU.max)
+        nc.vector.tensor_tensor(n1[:], a[:], f1[:], ALU.min)
+
+        m1_at3 = [sb.tile([P, HALF], F32, name="m1_at3_%d" % h) for h in range(2)]
+        w = [sb.tile([P, HALF], F32, name="w%d" % h) for h in range(2)]
+        for h in range(2):
+            nc.scalar.activation(m1_at3[h][:], m1[:].indirect(entries(idx3, h)), COPY)
+        for h in range(2):
+            nc.vector.tensor_tensor(w[h][:], n1[:].indirect(entries(idx4, h)), m1_at3[h][:], ALU.add)
+            nc.scalar.activation(f2[:].indirect(entries(idx5, h)), w[h][:], COPY)
+        n1_at = sb.tile([P, SLOTS], F32, name="n1_at")
+        nc.vector.tensor_copy(out=n1_at[:], in_=n1[:].indirect(idx[:]))
+
+        c2 = sb.tile([P, T], F32, name="c2")
+        nc.vector.tensor_tensor(c2[:], m1[:], f2[:], ALU.subtract)
+        c2_at3 = [sb.tile([P, HALF], F32, name="c2_at3_%d" % h) for h in range(2)]
+        nc.vector.tensor_copy(out=c2_at3[0][:], in_=c2[:].indirect(entries(idx3, 0)))
+        nc.scalar.activation(c2_at3[1][:], c2[:].indirect(entries(idx3, 1)), COPY)
+        for h, queue in enumerate((nc.sync, nc.scalar)):
+            y = sb.tile([P, HALF], F32, name="y%d" % h)
+            nc.vector.tensor_tensor(y[:], c2_at3[h][:], n1_at[:, slots(h)], ALU.max)
+            queue.dma_start(out=out[:, slots(h)], in_=y[:])

@@ -21,9 +21,8 @@ SLOTS = 512
 Q = 128
 QUADRANTS = 4
 LIVE = 4
-N_BANK = 256
 HALF = SLOTS // 2
-Q_VECTOR = 88
+BANK_COLUMNS = (slice(0, 256), slice(256, 512), slice(512, 768), slice(768, 896), slice(896, 1024))
 
 FLOPS = 2 * D * K * Q + 2 * K * Q * T + 2 * D * Q * T
 
@@ -35,10 +34,13 @@ def tile_attend_revisit_parts_kernel(tc, states, wq_words, wq_scales, cache_word
         sb = ctx.enter_context(tc.tile_pool(name="sb", bufs=1))
         ps = ctx.enter_context(tc.psum_pool(name="ps", bufs=1))
 
-        def stage_scales(queue, scales, width, name):
-            staged = sb.tile([LIVE, QUADRANTS, width // 4], I32, name=name)
-            queue.dma_start(out=staged[:], in_=scales[0].bitcast(I32).rearrange("(g r) c -> r g c", r=LIVE))
-            return staged
+        def stage_scales(queue, scales, width, loads, name):
+            blocks = QUADRANTS // loads
+            staged = sb.tile([P, blocks, width // 4], I32, align_bytes=64, name=name, tag=name)
+            rows = scales[0].bitcast(I32).rearrange("(u g r) c -> u r g c", u=loads, r=LIVE)
+            for u in range(loads):
+                queue.dma_start(out=staged[64 * u : 64 * u + LIVE], in_=rows[u])
+            return [staged[64 * (g // blocks) : 64 * (g // blocks) + LIVE, g % blocks, :] for g in range(QUADRANTS)]
 
         def zeroed_plane(width, name):
             plane = sb.tile([P, width], U8, align_bytes=64, name=name)
@@ -47,7 +49,7 @@ def tile_attend_revisit_parts_kernel(tc, states, wq_words, wq_scales, cache_word
 
         def spread_scales(plane, staged):
             for g in range(QUADRANTS):
-                nc.vector.tensor_copy(out=plane[32 * g : 32 * g + LIVE, :].bitcast(I32), in_=staged[:, g, :])
+                nc.vector.tensor_copy(out=plane[32 * g : 32 * g + LIVE, :].bitcast(I32),  in_=staged[g])
 
         def entries(lists, half):
             return lists[:, half * HALF // 16 : (half + 1) * HALF // 16]
@@ -55,15 +57,18 @@ def tile_attend_revisit_parts_kernel(tc, states, wq_words, wq_scales, cache_word
         def slots(half):
             return slice(half * HALF, (half + 1) * HALF)
 
-        wq_staged = stage_scales(nc.scalar, wq_scales, K, "wq_staged")
+        tags_plane = zeroed_plane(T, "tags_plane")
+        wq_staged = stage_scales(nc.scalar, wq_scales, K, 1, "wq_staged")
         states_raw = sb.tile([P, PACK, Q], F32, name="states_raw")
         nc.sync.dma_start(out=states_raw[:], in_=states.rearrange("(p j) q -> p j q", j=PACK))
         wq_codes = sb.tile([P, K], I32, align_bytes=64, name="wq_codes")
         nc.sync.dma_start(out=wq_codes[:], in_=wq_words[0].rearrange("p n t -> p (n t)").bitcast(I32))
-        tags_staged = stage_scales(nc.sync, tags_scales, T, "tags_staged")
-        cache_staged = stage_scales(nc.sync, cache_scales, T, "cache_staged")
+        for g in range(QUADRANTS):
+            nc.sync.dma_start(out=tags_plane[32 * g : 32 * g + LIVE, :].bitcast(I32),
+                              in_=tags_scales[0].bitcast(I32)[LIVE * g : LIVE * (g + 1), :])
         tags_codes = sb.tile([P, T], I32, align_bytes=64, name="tags_codes")
         nc.sync.dma_start(out=tags_codes[:], in_=tags_words[0].rearrange("p n t -> p (n t)").bitcast(I32))
+        cache_staged = stage_scales(nc.sync, cache_scales, T, 1, "cache_staged")
         cache_codes = sb.tile([P, 2 * T], U8, align_bytes=64, name="cache_codes")
         nc.sync.dma_start(out=cache_codes[:].bitcast(I32), in_=cache_words[0].bitcast(I32))
         lists = []
@@ -74,33 +79,40 @@ def tile_attend_revisit_parts_kernel(tc, states, wq_words, wq_scales, cache_word
         idx, idx2, idx3, idx4, idx5 = lists
 
         wq_plane = zeroed_plane(K, "wq_plane")
-        tags_plane = zeroed_plane(T, "tags_plane")
         cache_plane = zeroed_plane(T, "cache_plane")
         f1 = sb.tile([P, T], F32, name="f1")
         nc.vector.memset(f1[:], 0.0)
-        f2 = sb.tile([P, T], F32, name="f2")
-        nc.vector.memset(f2[:], 0.0)
+        f2_first = sb.tile([P, T], F32, name="f2_first")
+        nc.vector.memset(f2_first[:], 0.0)
 
         spread_scales(wq_plane, wq_staged)
 
-        states_bf = sb.tile([P, Q, PACK], BF16, align_bytes=64, name="states_bf")
-        lo, hi = slice(0, Q_VECTOR), slice(Q_VECTOR, Q)
-        nc.vector.tensor_copy(out=states_bf[:, lo, :].rearrange("p (c i) j -> p c j i", i=4),
-                              in_=states_raw[:, :, lo].rearrange("p j (c i) -> p c j i", i=4))
-        nc.scalar.activation(states_bf[:, hi, :].rearrange("p (c i) j -> p c j i", i=4),
-                             states_raw[:, :, hi].rearrange("p j (c i) -> p c j i", i=4), COPY)
+        states_bf = sb.tile([P, Q, PACK], BF16, align_bytes=64, name="states_bf", tag="states_bf_then_f2")
+        nc.scalar.activation(states_bf[:].rearrange("p (c i) j -> p c j i", i=4),
+                             states_raw[:].rearrange("p j (c i) -> p c j i", i=4), COPY)
 
         wq_plane_dealt = sb.tile([P, K], U8, align_bytes=64, name="wq_plane_dealt")
-        nc.vector.tensor_copy(out=wq_plane_dealt[:].rearrange("p (t c i) -> p c t i", t=PACK, i=16),
-                              in_=wq_plane[:].rearrange("p (c i t) -> p c t i", t=PACK, i=16))
+
+        def deal_scale_bytes(pair):
+            nc.vector.tensor_copy(
+                out=wq_plane_dealt[:].rearrange("p (t c i) -> p c t i", t=PACK, i=16)[:, :, pair, :],
+                in_=wq_plane[:].rearrange("p (c i t) -> p c t i", t=PACK, i=16)[:, :, pair, :])
+
+        deal_scale_bytes(slice(0, 2))
         wq_dealt = sb.tile([P, K], U32, align_bytes=64, name="wq_dealt")
-        nc.scalar.copy(wq_dealt[:].rearrange("p (t c i) -> p c t i", t=PACK, i=4),
-                       wq_codes[:].bitcast(U32).rearrange("p (c i t) -> p c t i", t=PACK, i=4))
+        for pair in (slice(0, 2), slice(2, 4)):
+            nc.scalar.copy(wq_dealt[:].rearrange("p (t c i) -> p c t i", t=PACK, i=4)[:, :, pair, :],
+                           wq_codes[:].bitcast(U32).rearrange("p (c i t) -> p c t i", t=PACK, i=4)[:, :, pair, :])
 
         states_codes = sb.tile([P, Q], U32, align_bytes=64, name="states_codes")
         states_plane = sb.tile([P, Q], U8, align_bytes=64, name="states_plane")
         nc.vector.quantize_mx(out=states_codes[:].bitcast(FP8X4), scales=states_plane[:],
                               in_=states_bf[:].rearrange("p q j -> p (q j)"))
+        deal_scale_bytes(slice(2, 4))
+
+        f2_second = sb.tile([P, T], F32, align_bytes=64, name="f2_second", tag="states_bf_then_f2")
+        nc.vector.memset(f2_second[:], 0.0)
+        f2 = (f2_first, f2_second)
 
         qv_ps = ps.tile([P, PACK, Q], F32, name="qv_ps")
         for t in range(PACK):
@@ -111,35 +123,32 @@ def tile_attend_revisit_parts_kernel(tc, states, wq_words, wq_scales, cache_word
         qv_bf = sb.tile([P, Q, PACK], BF16, align_bytes=64, name="qv_bf")
         nc.scalar.copy(qv_bf[:], qv_ps[:].rearrange("p t q -> p q t"))
 
-        spread_scales(tags_plane, tags_staged)
-        banks = [ps.tile([P, N_BANK], F32, name="a_ps%d" % b) for b in range(T // N_BANK)]
-        for b, bank in enumerate(banks):
-            cols = slice(b * N_BANK, (b + 1) * N_BANK)
+        banks = [ps.tile([P, cols.stop - cols.start], F32, name="a_ps%d" % cols.start) for cols in BANK_COLUMNS]
+        for bank, cols in zip(banks, BANK_COLUMNS):
             nc.tensor.matmul_mx(out=bank[:], lhsT=states_codes[:].bitcast(FP8X4), lhsT_scale=states_plane[:],
                                 rhs=tags_codes[:, cols].bitcast(FP8X4), rhs_scale=tags_plane[:, cols],
                                 start=True, stop=False)
         spread_scales(cache_plane, cache_staged)
 
-        qv_codes = sb.tile([P, Q], U32, align_bytes=64, name="qv_codes")
+        qv_codes = sb.tile([P, Q], U32, align_bytes=64, name="qv_codes", tag="cache_staged")
         qv_plane = sb.tile([P, Q], U8, align_bytes=64, name="qv_plane")
         nc.vector.quantize_mx(out=qv_codes[:].bitcast(FP8X4), scales=qv_plane[:],
                               in_=qv_bf[:].rearrange("p q t -> p (q t)"))
 
         a = sb.tile([P, T], F32, name="a")
-        for b, bank in enumerate(banks):
-            cols = slice(b * N_BANK, (b + 1) * N_BANK)
+        for b, (bank, cols) in enumerate(zip(banks, BANK_COLUMNS)):
             nc.tensor.matmul_mx(out=bank[:], lhsT=qv_codes[:].bitcast(FP8X4), lhsT_scale=qv_plane[:],
-                                rhs=cache_codes[:, 2 * b * N_BANK : 2 * (b + 1) * N_BANK].bitcast(FP4X4),
+                                rhs=cache_codes[:, 2 * cols.start : 2 * cols.stop].bitcast(FP4X4),
                                 rhs_scale=cache_plane[:, cols], start=False, stop=True)
-            if b % 2 == 0:
-                nc.scalar.copy(a[:, cols], bank[:])
-            else:
+            if b in (0, 2):
                 nc.vector.tensor_copy(out=a[:, cols], in_=bank[:])
+            else:
+                nc.scalar.copy(a[:, cols], bank[:])
 
-        picked = [sb.tile([P, HALF], F32, name="picked%d" % h) for h in range(2)]
-        for h in range(2):
-            nc.vector.tensor_copy(out=picked[h][:], in_=a[:].indirect(entries(idx, h)))
-            nc.scalar.activation(f1[:].indirect(entries(idx2, h)), picked[h][:], COPY)
+        picked = sb.tile([P, SLOTS], F32, name="picked")
+        nc.vector.tensor_copy(out=picked[:, slots(0)], in_=a[:].indirect(entries(idx, 0)))
+        nc.scalar.activation(picked[:, slots(1)], a[:].indirect(entries(idx, 1)), COPY)
+        nc.scalar.activation(f1[:].indirect(idx2[:]), picked[:], COPY)
 
         m1 = sb.tile([P, T], F32, name="m1")
         n1 = sb.tile([P, T], F32, name="n1")
@@ -152,16 +161,18 @@ def tile_attend_revisit_parts_kernel(tc, states, wq_words, wq_scales, cache_word
             nc.scalar.activation(m1_at3[h][:], m1[:].indirect(entries(idx3, h)), COPY)
         for h in range(2):
             nc.vector.tensor_tensor(w[h][:], n1[:].indirect(entries(idx4, h)), m1_at3[h][:], ALU.add)
-            nc.scalar.activation(f2[:].indirect(entries(idx5, h)), w[h][:], COPY)
+            nc.scalar.activation(f2[h][:].indirect(entries(idx5, h)), w[h][:], COPY)
         n1_at = sb.tile([P, SLOTS], F32, name="n1_at")
         nc.vector.tensor_copy(out=n1_at[:], in_=n1[:].indirect(idx[:]))
 
         c2 = sb.tile([P, T], F32, name="c2")
-        nc.vector.tensor_tensor(c2[:], m1[:], f2[:], ALU.subtract)
+        c2_part = sb.tile([P, T], F32, name="c2_part")
+        nc.vector.tensor_tensor(c2_part[:], m1[:], f2[0][:], ALU.subtract)
+        nc.vector.tensor_tensor(c2[:], c2_part[:], f2[1][:], ALU.subtract)
         c2_at3 = [sb.tile([P, HALF], F32, name="c2_at3_%d" % h) for h in range(2)]
         nc.vector.tensor_copy(out=c2_at3[0][:], in_=c2[:].indirect(entries(idx3, 0)))
         nc.scalar.activation(c2_at3[1][:], c2[:].indirect(entries(idx3, 1)), COPY)
-        for h, queue in enumerate((nc.sync, nc.scalar)):
+        for h, queue in ((1, nc.scalar), (0, nc.sync)):
             y = sb.tile([P, HALF], F32, name="y%d" % h)
             nc.vector.tensor_tensor(y[:], c2_at3[h][:], n1_at[:, slots(h)], ALU.max)
             queue.dma_start(out=out[:, slots(h)], in_=y[:])

@@ -21,6 +21,7 @@ SLOTS = 512
 Q = 128
 QUADRANTS = 4
 LIVE = 4
+TAGS_ROW = 4
 HALF = SLOTS // 2
 BANK_COLUMNS = (slice(0, 256), slice(256, 512), slice(512, 768), slice(768, 896), slice(896, 1024))
 
@@ -47,6 +48,11 @@ def tile_attend_revisit_parts_kernel(tc, states, wq_words, wq_scales, cache_word
             nc.vector.memset(plane[:].bitcast(I32), 0)
             return plane
 
+        def load_scale_rows(plane, scales, first):
+            for g in range(QUADRANTS):
+                nc.sync.dma_start(out=plane[32 * g + first : 32 * g + first + LIVE, :].bitcast(I32),
+                                  in_=scales[0].bitcast(I32)[LIVE * g : LIVE * (g + 1), :])
+
         def spread_scales(plane, staged):
             for g in range(QUADRANTS):
                 nc.vector.tensor_copy(out=plane[32 * g : 32 * g + LIVE, :].bitcast(I32),  in_=staged[g])
@@ -58,19 +64,18 @@ def tile_attend_revisit_parts_kernel(tc, states, wq_words, wq_scales, cache_word
             return slice(half * HALF, (half + 1) * HALF)
 
         tags_plane = zeroed_plane(T, "tags_plane")
+        cache_plane = zeroed_plane(T, "cache_plane")
         wq_staged = stage_scales(nc.scalar, wq_scales, K, 1, "wq_staged")
         states_raw = sb.tile([P, PACK, Q], F32, name="states_raw")
         nc.sync.dma_start(out=states_raw[:], in_=states.rearrange("(p j) q -> p j q", j=PACK))
         wq_codes = sb.tile([P, K], I32, align_bytes=64, name="wq_codes")
         nc.sync.dma_start(out=wq_codes[:], in_=wq_words[0].rearrange("p n t -> p (n t)").bitcast(I32))
-        for g in range(QUADRANTS):
-            nc.sync.dma_start(out=tags_plane[32 * g : 32 * g + LIVE, :].bitcast(I32),
-                              in_=tags_scales[0].bitcast(I32)[LIVE * g : LIVE * (g + 1), :])
+        load_scale_rows(tags_plane, tags_scales, TAGS_ROW)
         tags_codes = sb.tile([P, T], I32, align_bytes=64, name="tags_codes")
         nc.sync.dma_start(out=tags_codes[:], in_=tags_words[0].rearrange("p n t -> p (n t)").bitcast(I32))
-        cache_staged = stage_scales(nc.sync, cache_scales, T, 1, "cache_staged")
         cache_codes = sb.tile([P, 2 * T], U8, align_bytes=64, name="cache_codes")
         nc.sync.dma_start(out=cache_codes[:].bitcast(I32), in_=cache_words[0].bitcast(I32))
+        load_scale_rows(cache_plane, cache_scales, 0)
         lists = []
         for number, source in enumerate((offs, offs2, offs3, offs4, offs5)):
             held = sb.tile([P, SLOTS // 16], U16, name="list%d" % number)
@@ -79,7 +84,6 @@ def tile_attend_revisit_parts_kernel(tc, states, wq_words, wq_scales, cache_word
         idx, idx2, idx3, idx4, idx5 = lists
 
         wq_plane = zeroed_plane(K, "wq_plane")
-        cache_plane = zeroed_plane(T, "cache_plane")
         f1 = sb.tile([P, T], F32, name="f1")
         nc.vector.memset(f1[:], 0.0)
         f2_first = sb.tile([P, T], F32, name="f2_first")
@@ -126,11 +130,10 @@ def tile_attend_revisit_parts_kernel(tc, states, wq_words, wq_scales, cache_word
         banks = [ps.tile([P, cols.stop - cols.start], F32, name="a_ps%d" % cols.start) for cols in BANK_COLUMNS]
         for bank, cols in zip(banks, BANK_COLUMNS):
             nc.tensor.matmul_mx(out=bank[:], lhsT=states_codes[:].bitcast(FP8X4), lhsT_scale=states_plane[:],
-                                rhs=tags_codes[:, cols].bitcast(FP8X4), rhs_scale=tags_plane[:, cols],
+                                rhs=tags_codes[:, cols].bitcast(FP8X4), rhs_scale=tags_plane[TAGS_ROW:, cols],
                                 start=True, stop=False)
-        spread_scales(cache_plane, cache_staged)
 
-        qv_codes = sb.tile([P, Q], U32, align_bytes=64, name="qv_codes", tag="cache_staged")
+        qv_codes = sb.tile([P, Q], U32, align_bytes=64, name="qv_codes")
         qv_plane = sb.tile([P, Q], U8, align_bytes=64, name="qv_plane")
         nc.vector.quantize_mx(out=qv_codes[:].bitcast(FP8X4), scales=qv_plane[:],
                               in_=qv_bf[:].rearrange("p q t -> p (q t)"))

@@ -23,7 +23,7 @@ QUADRANTS = 4
 LIVE = 4
 TAGS_ROW = 4
 HALF = SLOTS // 2
-BANK_COLUMNS = (slice(0, 256), slice(256, 512), slice(512, 768), slice(768, 896), slice(896, 1024))
+BANK_COLUMNS = (slice(0, 256), slice(256, 384), slice(384, 640), slice(640, 768), slice(768, 896), slice(896, 1024))
 
 FLOPS = 2 * D * K * Q + 2 * K * Q * T + 2 * D * Q * T
 
@@ -159,14 +159,15 @@ def tile_attend_revisit_parts_kernel(tc, states, wq_words, wq_scales, cache_word
         nc.vector.tensor_tensor(n1[:], a[:], f1[:], ALU.min)
 
         m1_at3 = [sb.tile([P, HALF], F32, name="m1_at3_%d" % h) for h in range(2)]
-        w = [sb.tile([P, HALF], F32, name="w%d" % h) for h in range(2)]
+        w = [sb.tile([P, HALF], F32, name="w%d" % h, tag="w%d" % h) for h in range(2)]
         for h in range(2):
             nc.scalar.activation(m1_at3[h][:], m1[:].indirect(entries(idx3, h)), COPY)
         for h in range(2):
             nc.vector.tensor_tensor(w[h][:], n1[:].indirect(entries(idx4, h)), m1_at3[h][:], ALU.add)
             nc.scalar.activation(f2[h][:].indirect(entries(idx5, h)), w[h][:], COPY)
-        n1_at = sb.tile([P, SLOTS], F32, name="n1_at")
-        nc.vector.tensor_copy(out=n1_at[:], in_=n1[:].indirect(idx[:]))
+        n1_at = [sb.tile([P, HALF], F32, name="n1_at0", tag="w1"), sb.tile([P, HALF], F32, name="n1_at1")]
+        nc.vector.tensor_copy(out=n1_at[1][:], in_=n1[:].indirect(entries(idx, 1)))
+        nc.scalar.activation(n1_at[0][:], n1[:].indirect(entries(idx, 0)), COPY)
 
         c2 = sb.tile([P, T], F32, name="c2")
         c2_part = sb.tile([P, T], F32, name="c2_part")
@@ -177,5 +178,5 @@ def tile_attend_revisit_parts_kernel(tc, states, wq_words, wq_scales, cache_word
         nc.scalar.activation(c2_at3[1][:], c2[:].indirect(entries(idx3, 1)), COPY)
         for h, queue in ((1, nc.scalar), (0, nc.sync)):
             y = sb.tile([P, HALF], F32, name="y%d" % h)
-            nc.vector.tensor_tensor(y[:], c2_at3[h][:], n1_at[:, slots(h)], ALU.max)
+            nc.vector.tensor_tensor(y[:], c2_at3[h][:], n1_at[h][:], ALU.max)
             queue.dma_start(out=out[:, slots(h)], in_=y[:])

from contextlib import ExitStack

import concourse.mybir as mybir

F32 = mybir.dt.float32
BF16 = mybir.dt.bfloat16
I32 = mybir.dt.int32
U32 = mybir.dt.uint32
U16 = mybir.dt.uint16
U8 = mybir.dt.uint8
FP8X4 = mybir.dt.float8_e4m3fn_x4
FP4X4 = mybir.dt.float4_e2m1fn_x4
ALU = mybir.AluOpType
COPY = mybir.ActivationFunctionType.Copy

P = 128
PACK = 4
D = K = 512
T = 1024
SLOTS = 512
Q = 128
QUADRANTS = 4
LIVE = 4
TAGS_ROW = 4
HALF = SLOTS // 2
BANK_COLUMNS = (slice(0, 256), slice(256, 384), slice(384, 640), slice(640, 768), slice(768, 896), slice(896, 1024))

FLOPS = 2 * D * K * Q + 2 * K * Q * T + 2 * D * Q * T


def tile_attend_revisit_parts_kernel(tc, states, wq_words, wq_scales, cache_words, cache_scales,
                                      tags_words, tags_scales, offs, offs2, offs3, offs4, offs5, out):
    nc = tc.nc
    with ExitStack() as ctx:
        sb = ctx.enter_context(tc.tile_pool(name="sb", bufs=1))
        ps = ctx.enter_context(tc.psum_pool(name="ps", bufs=1))

        def stage_scales(queue, scales, width, loads, name):
            blocks = QUADRANTS // loads
            staged = sb.tile([P, blocks, width // 4], I32, align_bytes=64, name=name, tag=name)
            rows = scales[0].bitcast(I32).rearrange("(u g r) c -> u r g c", u=loads, r=LIVE)
            for u in range(loads):
                queue.dma_start(out=staged[64 * u : 64 * u + LIVE], in_=rows[u])
            return [staged[64 * (g // blocks) : 64 * (g // blocks) + LIVE, g % blocks, :] for g in range(QUADRANTS)]

        def zeroed_plane(width, name):
            plane = sb.tile([P, width], U8, align_bytes=64, name=name)
            nc.vector.memset(plane[:].bitcast(I32), 0)
            return plane

        def load_scale_rows(plane, scales, first):
            for g in range(QUADRANTS):
                nc.sync.dma_start(out=plane[32 * g + first : 32 * g + first + LIVE, :].bitcast(I32),
                                  in_=scales[0].bitcast(I32)[LIVE * g : LIVE * (g + 1), :])

        def spread_scales(plane, staged):
            for g in range(QUADRANTS):
                nc.vector.tensor_copy(out=plane[32 * g : 32 * g + LIVE, :].bitcast(I32),  in_=staged[g])

        def entries(lists, half):
            return lists[:, half * HALF // 16 : (half + 1) * HALF // 16]

        def slots(half):
            return slice(half * HALF, (half + 1) * HALF)

        tags_plane = zeroed_plane(T, "tags_plane")
        cache_plane = zeroed_plane(T, "cache_plane")
        wq_staged = stage_scales(nc.scalar, wq_scales, K, 1, "wq_staged")
        states_raw = sb.tile([P, PACK, Q], F32, name="states_raw")
        nc.sync.dma_start(out=states_raw[:], in_=states.rearrange("(p j) q -> p j q", j=PACK))
        wq_codes = sb.tile([P, K], I32, align_bytes=64, name="wq_codes")
        nc.sync.dma_start(out=wq_codes[:], in_=wq_words[0].rearrange("p n t -> p (n t)").bitcast(I32))
        load_scale_rows(tags_plane, tags_scales, TAGS_ROW)
        tags_codes = sb.tile([P, T], I32, align_bytes=64, name="tags_codes")
        nc.sync.dma_start(out=tags_codes[:], in_=tags_words[0].rearrange("p n t -> p (n t)").bitcast(I32))
        cache_codes = sb.tile([P, 2 * T], U8, align_bytes=64, name="cache_codes")
        nc.sync.dma_start(out=cache_codes[:].bitcast(I32), in_=cache_words[0].bitcast(I32))
        load_scale_rows(cache_plane, cache_scales, 0)
        lists = []
        for number, source in enumerate((offs, offs2, offs3, offs4, offs5)):
            held = sb.tile([P, SLOTS // 16], U16, name="list%d" % number)
            nc.sync.dma_start(held[:], source)
            lists.append(held)
        idx, idx2, idx3, idx4, idx5 = lists

        wq_plane = zeroed_plane(K, "wq_plane")
        f1 = sb.tile([P, T], F32, name="f1")
        nc.vector.memset(f1[:], 0.0)
        f2_first = sb.tile([P, T], F32, name="f2_first")
        nc.vector.memset(f2_first[:], 0.0)

        spread_scales(wq_plane, wq_staged)

        states_bf = sb.tile([P, Q, PACK], BF16, align_bytes=64, name="states_bf", tag="states_bf_then_f2")
        nc.scalar.activation(states_bf[:].rearrange("p (c i) j -> p c j i", i=4),
                             states_raw[:].rearrange("p j (c i) -> p c j i", i=4), COPY)

        wq_plane_dealt = sb.tile([P, K], U8, align_bytes=64, name="wq_plane_dealt")

        def deal_scale_bytes(pair):
            nc.vector.tensor_copy(
                out=wq_plane_dealt[:].rearrange("p (t c i) -> p c t i", t=PACK, i=16)[:, :, pair, :],
                in_=wq_plane[:].rearrange("p (c i t) -> p c t i", t=PACK, i=16)[:, :, pair, :])

        deal_scale_bytes(slice(0, 2))
        wq_dealt = sb.tile([P, K], U32, align_bytes=64, name="wq_dealt")
        for pair in (slice(0, 2), slice(2, 4)):
            nc.scalar.copy(wq_dealt[:].rearrange("p (t c i) -> p c t i", t=PACK, i=4)[:, :, pair, :],
                           wq_codes[:].bitcast(U32).rearrange("p (c i t) -> p c t i", t=PACK, i=4)[:, :, pair, :])

        states_codes = sb.tile([P, Q], U32, align_bytes=64, name="states_codes")
        states_plane = sb.tile([P, Q], U8, align_bytes=64, name="states_plane")
        nc.vector.quantize_mx(out=states_codes[:].bitcast(FP8X4), scales=states_plane[:],
                              in_=states_bf[:].rearrange("p q j -> p (q j)"))
        deal_scale_bytes(slice(2, 4))

        f2_second = sb.tile([P, T], F32, align_bytes=64, name="f2_second", tag="states_bf_then_f2")
        nc.vector.memset(f2_second[:], 0.0)
        f2 = (f2_first, f2_second)

        qv_ps = ps.tile([P, PACK, Q], F32, name="qv_ps")
        for t in range(PACK):
            cols = slice(t * P, (t + 1) * P)
            nc.tensor.matmul_mx(out=qv_ps[:, t, :], lhsT=wq_dealt[:, cols].bitcast(FP8X4),
                                lhsT_scale=wq_plane_dealt[:, cols], rhs=states_codes[:].bitcast(FP8X4),
                                rhs_scale=states_plane[:], start=True, stop=True)
        qv_bf = sb.tile([P, Q, PACK], BF16, align_bytes=64, name="qv_bf")
        nc.scalar.copy(qv_bf[:], qv_ps[:].rearrange("p t q -> p q t"))

        banks = [ps.tile([P, cols.stop - cols.start], F32, name="a_ps%d" % cols.start) for cols in BANK_COLUMNS]
        for bank, cols in zip(banks, BANK_COLUMNS):
            nc.tensor.matmul_mx(out=bank[:], lhsT=states_codes[:].bitcast(FP8X4), lhsT_scale=states_plane[:],
                                rhs=tags_codes[:, cols].bitcast(FP8X4), rhs_scale=tags_plane[TAGS_ROW:, cols],
                                start=True, stop=False)

        qv_codes = sb.tile([P, Q], U32, align_bytes=64, name="qv_codes")
        qv_plane = sb.tile([P, Q], U8, align_bytes=64, name="qv_plane")
        nc.vector.quantize_mx(out=qv_codes[:].bitcast(FP8X4), scales=qv_plane[:],
                              in_=qv_bf[:].rearrange("p q t -> p (q t)"))

        a = sb.tile([P, T], F32, name="a")
        for b, (bank, cols) in enumerate(zip(banks, BANK_COLUMNS)):
            nc.tensor.matmul_mx(out=bank[:], lhsT=qv_codes[:].bitcast(FP8X4), lhsT_scale=qv_plane[:],
                                rhs=cache_codes[:, 2 * cols.start : 2 * cols.stop].bitcast(FP4X4),
                                rhs_scale=cache_plane[:, cols], start=False, stop=True)
            if b in (0, 2):
                nc.vector.tensor_copy(out=a[:, cols], in_=bank[:])
            else:
                nc.scalar.copy(a[:, cols], bank[:])

        picked = sb.tile([P, SLOTS], F32, name="picked")
        nc.vector.tensor_copy(out=picked[:, slots(0)], in_=a[:].indirect(entries(idx, 0)))
        nc.scalar.activation(picked[:, slots(1)], a[:].indirect(entries(idx, 1)), COPY)
        nc.scalar.activation(f1[:].indirect(idx2[:]), picked[:], COPY)

        m1 = sb.tile([P, T], F32, name="m1")
        n1 = sb.tile([P, T], F32, name="n1")
        nc.vector.tensor_tensor(m1[:], a[:], f1[:], ALU.max)
        nc.vector.tensor_tensor(n1[:], a[:], f1[:], ALU.min)

        m1_at3 = [sb.tile([P, HALF], F32, name="m1_at3_%d" % h) for h in range(2)]
        w = [sb.tile([P, HALF], F32, name="w%d" % h, tag="w%d" % h) for h in range(2)]
        for h in range(2):
            nc.scalar.activation(m1_at3[h][:], m1[:].indirect(entries(idx3, h)), COPY)
        for h in range(2):
            nc.vector.tensor_tensor(w[h][:], n1[:].indirect(entries(idx4, h)), m1_at3[h][:], ALU.add)
            nc.scalar.activation(f2[h][:].indirect(entries(idx5, h)), w[h][:], COPY)
        n1_at = [sb.tile([P, HALF], F32, name="n1_at0", tag="w1"), sb.tile([P, HALF], F32, name="n1_at1")]
        nc.vector.tensor_copy(out=n1_at[1][:], in_=n1[:].indirect(entries(idx, 1)))
        nc.scalar.activation(n1_at[0][:], n1[:].indirect(entries(idx, 0)), COPY)

        c2 = sb.tile([P, T], F32, name="c2")
        c2_part = sb.tile([P, T], F32, name="c2_part")
        nc.vector.tensor_tensor(c2_part[:], m1[:], f2[0][:], ALU.subtract)
        nc.vector.tensor_tensor(c2[:], c2_part[:], f2[1][:], ALU.subtract)
        c2_at3 = [sb.tile([P, HALF], F32, name="c2_at3_%d" % h) for h in range(2)]
        nc.vector.tensor_copy(out=c2_at3[0][:], in_=c2[:].indirect(entries(idx3, 0)))
        nc.scalar.activation(c2_at3[1][:], c2[:].indirect(entries(idx3, 1)), COPY)
        for h, queue in ((1, nc.scalar), (0, nc.sync)):
            y = sb.tile([P, HALF], F32, name="y%d" % h)
            nc.vector.tensor_tensor(y[:], c2_at3[h][:], n1_at[h][:], ALU.max)
            queue.dma_start(out=out[:, slots(h)], in_=y[:])
